import numpy as np
import ml_dtypes


def mxq(x, axis, fmt="e4m3"):
    dtype, down = {"e4m3": (ml_dtypes.float8_e4m3fn, 7), "e5m2": (ml_dtypes.float8_e5m2, 14)}[fmt]
    v = np.moveaxis(np.asarray(x, np.float32).astype(ml_dtypes.bfloat16).astype(np.float64), axis, -1)
    blocks = v.reshape(v.shape[:-1] + (-1, 32))
    amax = np.abs(blocks).max(-1, keepdims=True)
    byte = np.maximum(np.where(amax > 0, np.frexp(amax)[1] - 1 + 127, 0) - down, 1)
    scale = np.exp2(byte - 127.0)
    codes = (blocks / scale).astype(np.float32).astype(dtype).astype(np.float64)
    return np.moveaxis((codes * scale).reshape(v.shape), -1, axis)


WIDE = False


def mx_kscale(k):
    if not WIDE:
        return np.ones(k)
    levels = np.array([10, -10, 5, -5, 0])
    if k % 512:
        return np.exp2(np.random.permutation(np.resize(levels, k // 32))).repeat(32)
    a = np.empty((k // 512, 16))
    for p in range(k // 512):
        a[p, :8] = np.random.permutation(np.resize(levels, 8))
        for g in range(8):
            far = levels[np.abs(levels - a[p, g]) >= 10]
            a[p, g + 8] = far[np.random.randint(len(far))]
    return np.exp2(a.ravel()).repeat(32)


def f64(x):
    return np.asarray(x).astype(np.float64)


def striped(idx):
    return np.tile(idx.reshape(-1, 16).T, (8, 1)).astype(np.uint16)


def unstriped(offs):
    return offs[:16].T.reshape(-1).astype(np.int64)


E2M1 = np.array([0.0, 0.5, 1.0, 1.5, 2.0, 3.0, 4.0, 6.0, -0.0, -0.5, -1.0, -1.5, -2.0, -3.0, -4.0, -6.0])


def pack_weight(w, fmt):
    k, n = w.shape
    w = f64(np.asarray(w, np.float32).astype(ml_dtypes.bfloat16)).reshape(k // 32, 32, n)
    amax = np.abs(w).max(1)
    if fmt == "e4m3":
        byte = np.frexp(amax)[1] - 1 + 127 - 7
    else:
        mant, ex = np.frexp(amax / 6.0)
        byte = np.where(mant > 0.5, ex, ex - 1) + 127
    byte = np.clip(np.where(amax > 0, byte, 1), 1, 254)
    scaled = (w * np.exp2(127.0 - byte)[:, None, :]).reshape(k, n).astype(np.float32)
    by_word = np.ascontiguousarray(scaled.reshape(k // 512, 128, 4, n).transpose(0, 1, 3, 2))
    if fmt == "e4m3":
        words = by_word.astype(ml_dtypes.float8_e4m3fn).view(np.uint8)
    else:
        c = by_word.astype(ml_dtypes.float4_e2m1fn).view(np.uint8) & 0xF
        words = (c[..., 0::2] | (c[..., 1::2] << 4)).reshape(k // 512, 128, 2 * n)
    return np.ascontiguousarray(words), np.ascontiguousarray(byte.astype(np.uint8).reshape(k // 512, 16, n))


def unpack_weight(words, scales, fmt):
    g, _, n = scales.shape
    words = np.ascontiguousarray(words).reshape(g, 128, n, -1)
    if fmt == "e4m3":
        vals = words.view(ml_dtypes.float8_e4m3fn).astype(np.float64)
    else:
        nib = np.empty((g, 128, n, 4), np.uint8)
        nib[..., 0::2] = words & 0xF
        nib[..., 1::2] = words >> 4
        vals = E2M1[nib]
    vals = vals * np.repeat(np.exp2(scales.astype(np.float64) - 127.0), 8, axis=1)[..., None]
    return vals.transpose(0, 1, 3, 2).reshape(g * 512, n)


def pack_table(v):
    words, scales = pack_weight(v, "e4m3")
    return np.concatenate([words.reshape(words.shape[0], -1), scales.reshape(scales.shape[0], -1)], axis=1)


def unpack_table(tab):
    g, t = tab.shape[0], tab.shape[1] // 528
    return unpack_weight(tab[:, :512 * t].reshape(g, 128, t, 4), tab[:, 512 * t:].reshape(g, 16, t), "e4m3")


K, L, M, T, S = 1536, 1536, 256, 512, 256


def setup_inputs():
    n = np.random.standard_normal
    s1 = mx_kscale(K)[:, None]
    s2 = mx_kscale(L)[:, None]
    p_w4 = pack_weight(n((K, M)) / np.sqrt(K) / s1, "e2m1")
    return {
        "tab": pack_table(n((K, T)) * s1),
        "w4_words": p_w4[0],
        "w4_scales": p_w4[1],
        "x": (n((L, S)) * s2).astype(np.float32),
        "u": (n((L, M)) / np.sqrt(L) / s2).astype(np.float32),
        "r": (n((256, 256))).astype(np.float32),
        "offs": striped(np.random.permutation(T)[:S]),
    }


def reference(tab, w4_words, w4_scales, x, u, r, offs):
    tab_ = unpack_table(tab)[:, unstriped(offs)]
    w4_ = unpack_weight(w4_words, w4_scales, "e2m1")
    x_ = mxq(f64(x), 0, "e4m3")
    u_ = mxq(f64(u), 0, "e4m3")
    y = w4_.T @ tab_ + u_.T @ x_
    return f64(r) + y

@@ -1,0 +1,203 @@
+from contextlib import ExitStack
+
+import concourse.mybir as mybir
+
+K, L, M, T, S = 1536, 1536, 256, 512, 256
+P = 128
+PACK = 4
+PASSES = 3
+FLOPS = 2 * (K + L) * M * S
+
+F32 = mybir.dt.float32
+BF16 = mybir.dt.bfloat16
+I32 = mybir.dt.int32
+U32 = mybir.dt.uint32
+U16 = mybir.dt.uint16
+U8 = mybir.dt.uint8
+FP8X4 = mybir.dt.float8_e4m3fn_x4
+FP4X4 = mybir.dt.float4_e2m1fn_x4
+ADD = mybir.AluOpType.add
+
+
+def tile_list_tabx_res_kernel(tc, tab, w4_words, w4_scales, x, u, r, offs, out):
+    nc = tc.nc
+    with ExitStack() as ctx:
+        pool = ctx.enter_context(tc.tile_pool(name="keep", bufs=1))
+        psum = ctx.enter_context(tc.psum_pool(name="psum", bufs=1))
+
+        def sb(name, shape, dtype):
+            return pool.tile(shape, dtype, name=name, align_bytes=64)
+
+        offsets = pool.tile([P, S // 16], U16, name="offsets")
+        tw = [sb(f"tab_words{a}", [P, T], I32) for a in range(PASSES)]
+        ts = sb("tab_scales", [P, PASSES * T], U8)
+        ww = sb("w4_words_sb", [P, PASSES, 2 * M], U8)
+        ws = sb("w4_scales_sb", [P, PASSES * M], U8)
+        hbm = {"x": x, "u": u}
+        pieces = [("x", 0, 0, S), ("u", 0, 0, S), ("x", 1, 0, S), ("u", 1, 0, S), ("x", 2, 0, S), ("u", 2, 0, P), ("u", 2, P, S)]
+        raw = {}
+        grouped = {}
+        codes = {}
+        scales = {}
+        for v, a, lo, hi in pieces:
+            raw[v, a, lo] = sb(f"{v}_raw{a}_{lo}", [P, PACK, hi - lo], F32)
+            grouped[v, a, lo] = sb(f"{v}_grouped{a}_{lo}", [P, hi - lo, PACK], BF16)
+            codes[v, a, lo] = sb(f"{v}_codes{a}_{lo}", [P, hi - lo], U32)
+            scales[v, a, lo] = sb(f"{v}_scales{a}_{lo}", [P, hi - lo], U8)
+        gw = [sb(f"picked_words{a}", [P, S], U32) for a in range(PASSES)]
+        gs = [sb(f"picked_scales{a}", [P, S], U8) for a in range(PASSES)]
+        rsb = sb("r_sb", [P, 2, S], F32)
+        rs = [rsb[:, m, :] for m in range(2)]
+        res = [sb(f"result{m}", [P, S], F32) for m in range(2)]
+        acc = {(m, h): psum.tile([P, P], F32, name=f"acc{m}{h}") for m in range(2) for h in range(2)}
+
+        nc.sync.dma_start(offsets[:], offs)
+
+        nc.vector.memset(ts[:].bitcast(I32), 0)
+        nc.vector.memset(ws[:].bitcast(I32), 0)
+
+        def load_tab(a, q=nc.sync):
+            q.dma_start(tw[a][:], tab[a, 0 : 4 * P * T].rearrange("(p b) -> p b", p=P).bitcast(I32))
+
+        def load_raw(v, a, lo=0, hi=S, q=nc.sync):
+            q.dma_start(
+                raw[v, a, lo][:],
+                hbm[v][4 * P * a : 4 * P * (a + 1), lo:hi].rearrange("(p j) s -> p j s", j=PACK),
+            )
+
+        tab_scale_rows = tab[:, 4 * P * T :].rearrange("a (quad row t) -> row quad a t", quad=4, row=4)
+        w4_scale_rows = w4_scales.rearrange("a (quad row) n -> row quad a n", row=4)
+
+        def load_tab_scales(queue):
+            for row in range(4):
+                queue.dma_start(
+                    ts[row : P : 32, :].rearrange("q (a t) -> q a t", a=PASSES).bitcast(I32),
+                    tab_scale_rows[row].bitcast(I32),
+                )
+
+        def load_w4_scales(queue):
+            for row in range(4):
+                queue.dma_start(
+                    ws[row : P : 32, :].rearrange("q (a n) -> q a n", a=PASSES).bitcast(I32),
+                    w4_scale_rows[row].bitcast(I32),
+                )
+
+        def load_w4(lo, hi, queue=nc.sync):
+            queue.dma_start(ww[:, lo:hi, :].bitcast(I32), w4_words[lo:hi].rearrange("a p b -> p a b").bitcast(I32))
+
+        def load_r(queue=nc.sync):
+            queue.dma_start(rsb[:], r.rearrange("(m p) j -> p m j", p=P))
+
+        load_tab(0)
+        load_raw("x", 0)
+        load_tab_scales(nc.sync)
+        load_raw("u", 0)
+        load_tab(1)
+        load_raw("x", 1)
+        load_raw("u", 1)
+        load_w4_scales(nc.sync)
+        load_w4(0, 2)
+        load_tab(2)
+        load_raw("x", 2)
+        load_raw("u", 2, 0, P)
+        load_raw("u", 2, P, S)
+        load_w4(2, 3)
+        load_r()
+
+        def interleave(engine, v, a, base, lo, hi):
+            dst = grouped[v, a, base][:, lo:hi, :].rearrange("p (c i) t -> p c t i", i=4)
+            src = raw[v, a, base][:, :, lo:hi].rearrange("p t (c i) -> p c t i", i=4)
+            if engine == "S":
+                nc.scalar.copy(dst, src)
+            else:
+                nc.vector.tensor_copy(dst, src)
+
+        def quantize(v, a, base=0):
+            nc.vector.quantize_mx(
+                out=codes[v, a, base][:].bitcast(FP8X4),
+                scales=scales[v, a, base][:],
+                in_=grouped[v, a, base][:].rearrange("p s t -> p (s t)"),
+            )
+
+        def pick_words(a, lo=0, hi=S):
+            nc.vector.tensor_copy(gw[a][:, lo:hi], tw[a][:].bitcast(U32).indirect(offsets[:, lo // 16 : hi // 16]))
+
+        def pick_scales(a):
+            nc.vector.tensor_copy(gs[a][:], ts[:, T * a : T * (a + 1)].indirect(offsets[:]))
+
+        def own(a, m, h, start, stop):
+            if ("u", a, P) in codes:
+                lc, ls = codes["u", a, P * m][:], scales["u", a, P * m][:]
+            else:
+                mc = slice(P * m, P * (m + 1))
+                lc, ls = codes["u", a, 0][:, mc], scales["u", a, 0][:, mc]
+            hc = slice(P * h, P * (h + 1))
+            nc.tensor.matmul_mx(
+                out=acc[m, h][:],
+                lhsT=lc.bitcast(FP8X4), lhsT_scale=ls,
+                rhs=codes["x", a, 0][:, hc].bitcast(FP8X4), rhs_scale=scales["x", a, 0][:, hc],
+                start=start, stop=stop,
+            )
+
+        def memory(a, m, h, start, stop):
+            hc = slice(P * h, P * (h + 1))
+            nc.tensor.matmul_mx(
+                out=acc[m, h][:],
+                lhsT=ww[:, a, 2 * P * m : 2 * P * (m + 1)].bitcast(FP4X4),
+                lhsT_scale=ws[:, M * a + P * m : M * a + P * (m + 1)],
+                rhs=gw[a][:, hc].bitcast(FP8X4), rhs_scale=gs[a][:, hc],
+                start=start, stop=stop,
+            )
+
+        def add(m, h):
+            hc = slice(P * h, P * (h + 1))
+            nc.vector.tensor_tensor(res[m][:, hc], acc[m, h][:], rs[m][:, hc], ADD)
+
+        def store(m, queue):
+            queue.dma_start(out[P * m : P * (m + 1), :], res[m][:])
+
+        four = [(m, h) for m in range(2) for h in range(2)]
+        pick_words(0)
+        interleave("S", "x", 0, 0, 0, S)
+        pick_scales(0)
+        pick_scales(1)
+        pick_scales(2)
+        quantize("x", 0)
+        interleave("S", "u", 0, 0, 0, S)
+        pick_words(1)
+        quantize("u", 0)
+        for m, h in four:
+            own(0, m, h, True, False)
+        interleave("S", "x", 1, 0, 0, 192)
+        interleave("V", "x", 1, 0, 192, S)
+        quantize("x", 1)
+        for m, h in four:
+            memory(0, m, h, False, False)
+        for m, h in four:
+            memory(1, m, h, False, False)
+        interleave("S", "u", 1, 0, 0, 192)
+        interleave("V", "u", 1, 0, 192, S)
+        quantize("u", 1)
+        for m, h in four:
+            own(1, m, h, False, False)
+        pick_words(2)
+        interleave("S", "x", 2, 0, 0, 96)
+        interleave("V", "x", 2, 0, 96, S)
+        for m, h in four:
+            memory(2, m, h, False, False)
+        interleave("S", "u", 2, 0, 0, P)
+        quantize("x", 2)
+        interleave("S", "u", 2, P, 0, 40)
+        interleave("V", "u", 2, P, 40, P)
+        quantize("u", 2, 0)
+        own(2, 0, 0, False, True)
+        own(2, 0, 1, False, True)
+        quantize("u", 2, P)
+        own(2, 1, 0, False, True)
+        own(2, 1, 1, False, True)
+        add(0, 0)
+        add(0, 1)
+        store(0, nc.sync)
+        add(1, 0)
+        add(1, 1)
+        store(1, nc.sync)

@@ -51,8 +51,6 @@ def tile_list_tabx_res_kernel(tc, tab, w4_words, w4_scales, x, u, r, offs, out):
         res = [sb(f"result{m}", [P, S], F32) for m in range(2)]
         acc = {(m, h): psum.tile([P, P], F32, name=f"acc{m}{h}") for m in range(2) for h in range(2)}
 
-        nc.sync.dma_start(offsets[:], offs)
-
         nc.vector.memset(ts[:].bitcast(I32), 0)
         nc.vector.memset(ws[:].bitcast(I32), 0)
 
@@ -89,15 +87,16 @@ def tile_list_tabx_res_kernel(tc, tab, w4_words, w4_scales, x, u, r, offs, out):
             queue.dma_start(rsb[:], r.rearrange("(m p) j -> p m j", p=P))
 
         load_tab(0)
+        nc.sync.dma_start(offsets[:], offs)
         load_raw("x", 0)
         load_tab_scales(nc.sync)
         load_raw("u", 0)
         load_tab(1)
         load_raw("x", 1)
+        load_tab(2)
         load_raw("u", 1)
         load_w4_scales(nc.sync)
         load_w4(0, 2)
-        load_tab(2)
         load_raw("x", 2)
         load_raw("u", 2, 0, P)
         load_raw("u", 2, P, S)
@@ -171,16 +170,16 @@ def tile_list_tabx_res_kernel(tc, tab, w4_words, w4_scales, x, u, r, offs, out):
         interleave("S", "x", 1, 0, 0, 192)
         interleave("V", "x", 1, 0, 192, S)
         quantize("x", 1)
+        pick_words(2)
         for m, h in four:
             memory(0, m, h, False, False)
         for m, h in four:
             memory(1, m, h, False, False)
-        interleave("S", "u", 1, 0, 0, 192)
-        interleave("V", "u", 1, 0, 192, S)
+        interleave("S", "u", 1, 0, 0, 144)
+        interleave("V", "u", 1, 0, 144, S)
         quantize("u", 1)
         for m, h in four:
             own(1, m, h, False, False)
-        pick_words(2)
         interleave("S", "x", 2, 0, 0, 96)
         interleave("V", "x", 2, 0, 96, S)
         for m, h in four:

@@ -34,7 +34,7 @@ def tile_list_tabx_res_kernel(tc, tab, w4_words, w4_scales, x, u, r, offs, out):
         ww = sb("w4_words_sb", [P, PASSES, 2 * M], U8)
         ws = sb("w4_scales_sb", [P, PASSES * M], U8)
         hbm = {"x": x, "u": u}
-        pieces = [("x", 0, 0, S), ("u", 0, 0, S), ("x", 1, 0, S), ("u", 1, 0, S), ("x", 2, 0, S), ("u", 2, 0, P), ("u", 2, P, S)]
+        pieces = [("x", 0, 0, S), ("u", 0, 0, S), ("x", 1, 0, S), ("u", 1, 0, S), ("u", 2, 0, S), ("x", 2, 0, P), ("x", 2, P, S)]
         raw = {}
         grouped = {}
         codes = {}
@@ -48,7 +48,7 @@ def tile_list_tabx_res_kernel(tc, tab, w4_words, w4_scales, x, u, r, offs, out):
         gs = [sb(f"picked_scales{a}", [P, S], U8) for a in range(PASSES)]
         rsb = sb("r_sb", [P, 2, S], F32)
         rs = [rsb[:, m, :] for m in range(2)]
-        res = [sb(f"result{m}", [P, S], F32) for m in range(2)]
+        res = [sb(f"result{h}", [P, 2, P], F32) for h in range(2)]
         acc = {(m, h): psum.tile([P, P], F32, name=f"acc{m}{h}") for m in range(2) for h in range(2)}
 
         nc.vector.memset(ts[:].bitcast(I32), 0)
@@ -97,9 +97,9 @@ def tile_list_tabx_res_kernel(tc, tab, w4_words, w4_scales, x, u, r, offs, out):
         load_raw("u", 1)
         load_w4_scales(nc.sync)
         load_w4(0, 2)
-        load_raw("x", 2)
-        load_raw("u", 2, 0, P)
-        load_raw("u", 2, P, S)
+        load_raw("u", 2)
+        load_raw("x", 2, 0, P)
+        load_raw("x", 2, P, S)
         load_w4(2, 3)
         load_r()
 
@@ -124,17 +124,19 @@ def tile_list_tabx_res_kernel(tc, tab, w4_words, w4_scales, x, u, r, offs, out):
         def pick_scales(a):
             nc.vector.tensor_copy(gs[a][:], ts[:, T * a : T * (a + 1)].indirect(offsets[:]))
 
+        def operand(v, a, half):
+            if (v, a, P) in codes:
+                return codes[v, a, P * half][:], scales[v, a, P * half][:]
+            cols = slice(P * half, P * (half + 1))
+            return codes[v, a, 0][:, cols], scales[v, a, 0][:, cols]
+
         def own(a, m, h, start, stop):
-            if ("u", a, P) in codes:
-                lc, ls = codes["u", a, P * m][:], scales["u", a, P * m][:]
-            else:
-                mc = slice(P * m, P * (m + 1))
-                lc, ls = codes["u", a, 0][:, mc], scales["u", a, 0][:, mc]
-            hc = slice(P * h, P * (h + 1))
+            lc, ls = operand("u", a, m)
+            rc, rscale = operand("x", a, h)
             nc.tensor.matmul_mx(
                 out=acc[m, h][:],
                 lhsT=lc.bitcast(FP8X4), lhsT_scale=ls,
-                rhs=codes["x", a, 0][:, hc].bitcast(FP8X4), rhs_scale=scales["x", a, 0][:, hc],
+                rhs=rc.bitcast(FP8X4), rhs_scale=rscale,
                 start=start, stop=stop,
             )
 
@@ -150,10 +152,10 @@ def tile_list_tabx_res_kernel(tc, tab, w4_words, w4_scales, x, u, r, offs, out):
 
         def add(m, h):
             hc = slice(P * h, P * (h + 1))
-            nc.vector.tensor_tensor(res[m][:, hc], acc[m, h][:], rs[m][:, hc], ADD)
+            nc.vector.tensor_tensor(res[h][:, m, :], acc[m, h][:], rs[m][:, hc], ADD)
 
-        def store(m, queue):
-            queue.dma_start(out[P * m : P * (m + 1), :], res[m][:])
+        def store(h, queue):
+            queue.dma_start(out[:, P * h : P * (h + 1)].rearrange("(m p) j -> p m j", p=P), res[h][:])
 
         four = [(m, h) for m in range(2) for h in range(2)]
         pick_words(0)
@@ -180,23 +182,23 @@ def tile_list_tabx_res_kernel(tc, tab, w4_words, w4_scales, x, u, r, offs, out):
         quantize("u", 1)
         for m, h in four:
             own(1, m, h, False, False)
-        interleave("S", "x", 2, 0, 0, 96)
-        interleave("V", "x", 2, 0, 96, S)
+        interleave("S", "u", 2, 0, 0, 96)
+        interleave("V", "u", 2, 0, 96, S)
         for m, h in four:
             memory(2, m, h, False, False)
-        interleave("S", "u", 2, 0, 0, P)
-        quantize("x", 2)
-        interleave("S", "u", 2, P, 0, 40)
-        interleave("V", "u", 2, P, 40, P)
-        quantize("u", 2, 0)
+        interleave("S", "x", 2, 0, 0, P)
+        quantize("u", 2)
+        interleave("S", "x", 2, P, 0, 40)
+        interleave("V", "x", 2, P, 40, P)
+        quantize("x", 2, 0)
         own(2, 0, 0, False, True)
-        own(2, 0, 1, False, True)
-        quantize("u", 2, P)
         own(2, 1, 0, False, True)
+        quantize("x", 2, P)
+        own(2, 0, 1, False, True)
         own(2, 1, 1, False, True)
         add(0, 0)
-        add(0, 1)
-        store(0, nc.sync)
         add(1, 0)
+        store(0, nc.sync)
+        add(0, 1)
         add(1, 1)
         store(1, nc.sync)

@@ -34,7 +34,7 @@ def tile_list_tabx_res_kernel(tc, tab, w4_words, w4_scales, x, u, r, offs, out):
         ww = sb("w4_words_sb", [P, PASSES, 2 * M], U8)
         ws = sb("w4_scales_sb", [P, PASSES * M], U8)
         hbm = {"x": x, "u": u}
-        pieces = [("x", 0, 0, S), ("u", 0, 0, S), ("x", 1, 0, S), ("u", 1, 0, S), ("u", 2, 0, S), ("x", 2, 0, P), ("x", 2, P, S)]
+        pieces = [("x", 0, 0, S), ("u", 0, 0, S), ("x", 1, 0, S), ("u", 1, 0, P), ("u", 1, P, S), ("x", 2, 0, P), ("x", 2, P, S), ("u", 2, 0, P), ("u", 2, P, S)]
         raw = {}
         grouped = {}
         codes = {}
@@ -46,13 +46,12 @@ def tile_list_tabx_res_kernel(tc, tab, w4_words, w4_scales, x, u, r, offs, out):
             scales[v, a, lo] = sb(f"{v}_scales{a}_{lo}", [P, hi - lo], U8)
         gw = [sb(f"picked_words{a}", [P, S], U32) for a in range(PASSES)]
         gs = [sb(f"picked_scales{a}", [P, S], U8) for a in range(PASSES)]
-        rsb = sb("r_sb", [P, 2, S], F32)
-        rs = [rsb[:, m, :] for m in range(2)]
-        res = [sb(f"result{h}", [P, 2, P], F32) for h in range(2)]
+        rs = [sb(f"r_sb{m}", [P, S], F32) for m in range(2)]
+        res = [sb(f"result{m}", [P, S], F32) for m in range(2)]
         acc = {(m, h): psum.tile([P, P], F32, name=f"acc{m}{h}") for m in range(2) for h in range(2)}
 
         nc.vector.memset(ts[:].bitcast(I32), 0)
-        nc.vector.memset(ws[:].bitcast(I32), 0)
+        nc.gpsimd.memset(ws[:].bitcast(I32), 0)
 
         def load_tab(a, q=nc.sync):
             q.dma_start(tw[a][:], tab[a, 0 : 4 * P * T].rearrange("(p b) -> p b", p=P).bitcast(I32))
@@ -84,8 +83,10 @@ def tile_list_tabx_res_kernel(tc, tab, w4_words, w4_scales, x, u, r, offs, out):
             queue.dma_start(ww[:, lo:hi, :].bitcast(I32), w4_words[lo:hi].rearrange("a p b -> p a b").bitcast(I32))
 
         def load_r(queue=nc.sync):
-            queue.dma_start(rsb[:], r.rearrange("(m p) j -> p m j", p=P))
+            for m in range(2):
+                queue.dma_start(rs[m][:], r[P * m : P * (m + 1), :])
 
+        load_w4_scales(nc.gpsimd)
         load_tab(0)
         nc.sync.dma_start(offsets[:], offs)
         load_raw("x", 0)
@@ -94,12 +95,14 @@ def tile_list_tabx_res_kernel(tc, tab, w4_words, w4_scales, x, u, r, offs, out):
         load_tab(1)
         load_raw("x", 1)
         load_tab(2)
-        load_raw("u", 1)
-        load_w4_scales(nc.sync)
-        load_w4(0, 2)
-        load_raw("u", 2)
+        load_raw("u", 1, 0, P)
+        load_raw("u", 1, P, S)
+        load_w4(0, 1)
+        load_w4(1, 2)
+        load_raw("u", 2, 0, P)
         load_raw("x", 2, 0, P)
         load_raw("x", 2, P, S)
+        load_raw("u", 2, P, S)
         load_w4(2, 3)
         load_r()
 
@@ -152,10 +155,10 @@ def tile_list_tabx_res_kernel(tc, tab, w4_words, w4_scales, x, u, r, offs, out):
 
         def add(m, h):
             hc = slice(P * h, P * (h + 1))
-            nc.vector.tensor_tensor(res[h][:, m, :], acc[m, h][:], rs[m][:, hc], ADD)
+            nc.vector.tensor_tensor(res[m][:, hc], acc[m, h][:], rs[m][:, hc], ADD)
 
-        def store(h, queue):
-            queue.dma_start(out[:, P * h : P * (h + 1)].rearrange("(m p) j -> p m j", p=P), res[h][:])
+        def store(m, queue):
+            queue.dma_start(out[P * m : P * (m + 1), :], res[m][:])
 
         four = [(m, h) for m in range(2) for h in range(2)]
         pick_words(0)
@@ -177,28 +180,32 @@ def tile_list_tabx_res_kernel(tc, tab, w4_words, w4_scales, x, u, r, offs, out):
             memory(0, m, h, False, False)
         for m, h in four:
             memory(1, m, h, False, False)
-        interleave("S", "u", 1, 0, 0, 144)
-        interleave("V", "u", 1, 0, 144, S)
-        quantize("u", 1)
+        interleave("S", "u", 1, 0, 0, P)
+        interleave("V", "u", 1, P, 0, P)
+        quantize("u", 1, 0)
+        quantize("u", 1, P)
         for m, h in four:
             own(1, m, h, False, False)
-        interleave("S", "u", 2, 0, 0, 96)
-        interleave("V", "u", 2, 0, 96, S)
-        for m, h in four:
-            memory(2, m, h, False, False)
-        interleave("S", "x", 2, 0, 0, P)
-        quantize("u", 2)
-        interleave("S", "x", 2, P, 0, 40)
-        interleave("V", "x", 2, P, 40, P)
+        interleave("S", "u", 2, 0, 0, P)
+        interleave("V", "x", 2, 0, 0, P)
+        quantize("u", 2, 0)
         quantize("x", 2, 0)
-        own(2, 0, 0, False, True)
-        own(2, 1, 0, False, True)
+        own(2, 0, 0, False, False)
+        interleave("S", "x", 2, P, 0, P)
+        interleave("S", "u", 2, P, 0, 40)
+        interleave("V", "u", 2, P, 40, P)
         quantize("x", 2, P)
+        memory(2, 0, 0, False, True)
+        memory(2, 0, 1, False, False)
+        memory(2, 1, 0, False, False)
+        memory(2, 1, 1, False, False)
         own(2, 0, 1, False, True)
+        quantize("u", 2, P)
+        own(2, 1, 0, False, True)
         own(2, 1, 1, False, True)
         add(0, 0)
-        add(1, 0)
-        store(0, nc.sync)
         add(0, 1)
+        store(0, nc.sync)
+        add(1, 0)
         add(1, 1)
         store(1, nc.sync)

@@ -50,8 +50,8 @@ def tile_list_tabx_res_kernel(tc, tab, w4_words, w4_scales, x, u, r, offs, out):
         res = [sb(f"result{m}", [P, S], F32) for m in range(2)]
         acc = {(m, h): psum.tile([P, P], F32, name=f"acc{m}{h}") for m in range(2) for h in range(2)}
 
+        nc.vector.memset(ws[:].bitcast(I32), 0)
         nc.vector.memset(ts[:].bitcast(I32), 0)
-        nc.gpsimd.memset(ws[:].bitcast(I32), 0)
 
         def load_tab(a, q=nc.sync):
             q.dma_start(tw[a][:], tab[a, 0 : 4 * P * T].rearrange("(p b) -> p b", p=P).bitcast(I32))
@@ -172,8 +172,7 @@ def tile_list_tabx_res_kernel(tc, tab, w4_words, w4_scales, x, u, r, offs, out):
         quantize("u", 0)
         for m, h in four:
             own(0, m, h, True, False)
-        interleave("S", "x", 1, 0, 0, 192)
-        interleave("V", "x", 1, 0, 192, S)
+        interleave("S", "x", 1, 0, 0, S)
         quantize("x", 1)
         pick_words(2)
         for m, h in four:
@@ -181,7 +180,7 @@ def tile_list_tabx_res_kernel(tc, tab, w4_words, w4_scales, x, u, r, offs, out):
         for m, h in four:
             memory(1, m, h, False, False)
         interleave("S", "u", 1, 0, 0, P)
-        interleave("V", "u", 1, P, 0, P)
+        interleave("S", "u", 1, P, 0, P)
         quantize("u", 1, 0)
         quantize("u", 1, P)
         for m, h in four:

@@ -29,82 +29,73 @@ def tile_list_tabx_res_kernel(tc, tab, w4_words, w4_scales, x, u, r, offs, out):
             return pool.tile(shape, dtype, name=name, align_bytes=64)
 
         offsets = pool.tile([P, S // 16], U16, name="offsets")
-        tw = [sb(f"tab_words{a}", [P, T], I32) for a in range(PASSES)]
         ts = sb("tab_scales", [P, PASSES * T], U8)
         ww = sb("w4_words_sb", [P, PASSES, 2 * M], U8)
         ws = sb("w4_scales_sb", [P, PASSES * M], U8)
+        gw = [sb(f"picked_words{a}", [P, S], U32) for a in range(PASSES)]
+        gs = [sb(f"picked_scales{a}", [P, S], U8) for a in range(PASSES)]
+        rs = sb("r_sb", [P, 2, S], F32)
+        res = [sb(f"result{m}", [P, S], F32) for m in range(2)]
+        acc = {(m, h): psum.tile([P, P], F32, name=f"acc{m}{h}") for m in range(2) for h in range(2)}
         hbm = {"x": x, "u": u}
-        pieces = [("x", 0, 0, S), ("u", 0, 0, S), ("x", 1, 0, S), ("u", 1, 0, P), ("u", 1, P, S), ("x", 2, 0, P), ("x", 2, P, S), ("u", 2, 0, P), ("u", 2, P, S)]
+        tw = {}
         raw = {}
         grouped = {}
         codes = {}
         scales = {}
-        for v, a, lo, hi in pieces:
-            raw[v, a, lo] = sb(f"{v}_raw{a}_{lo}", [P, PACK, hi - lo], F32)
+
+        def load_tab(lo, hi):
+            words = sb(f"tab_words{lo}", [P, hi - lo, T], I32)
+            nc.sync.dma_start(
+                words[:], tab[lo:hi, 0 : 4 * P * T].rearrange("a (p b) -> p a b", p=P).bitcast(I32)
+            )
+            for a in range(lo, hi):
+                tw[a] = words[:, a - lo, :]
+
+        def make_piece(v, a, lo, hi):
             grouped[v, a, lo] = sb(f"{v}_grouped{a}_{lo}", [P, hi - lo, PACK], BF16)
             codes[v, a, lo] = sb(f"{v}_codes{a}_{lo}", [P, hi - lo], U32)
             scales[v, a, lo] = sb(f"{v}_scales{a}_{lo}", [P, hi - lo], U8)
-        gw = [sb(f"picked_words{a}", [P, S], U32) for a in range(PASSES)]
-        gs = [sb(f"picked_scales{a}", [P, S], U8) for a in range(PASSES)]
-        rs = [sb(f"r_sb{m}", [P, S], F32) for m in range(2)]
-        res = [sb(f"result{m}", [P, S], F32) for m in range(2)]
-        acc = {(m, h): psum.tile([P, P], F32, name=f"acc{m}{h}") for m in range(2) for h in range(2)}
 
-        nc.vector.memset(ws[:].bitcast(I32), 0)
-        nc.vector.memset(ts[:].bitcast(I32), 0)
-
-        def load_tab(a, q=nc.sync):
-            q.dma_start(tw[a][:], tab[a, 0 : 4 * P * T].rearrange("(p b) -> p b", p=P).bitcast(I32))
-
-        def load_raw(v, a, lo=0, hi=S, q=nc.sync):
-            q.dma_start(
-                raw[v, a, lo][:],
-                hbm[v][4 * P * a : 4 * P * (a + 1), lo:hi].rearrange("(p j) s -> p j s", j=PACK),
+        def load_passes(v, lo, hi):
+            rows = sb(f"{v}_raw{lo}", [P, hi - lo, PACK * S], F32)
+            nc.sync.dma_start(
+                rows[:], hbm[v][4 * P * lo : 4 * P * hi, :].rearrange("(a p j) s -> p a (j s)", p=P, j=PACK)
             )
+            for a in range(lo, hi):
+                raw[v, a, 0] = rows[:, a - lo, :].rearrange("p (j s) -> p j s", j=PACK)
+                make_piece(v, a, 0, S)
+
+        def load_columns(v, a, lo, hi):
+            rows = sb(f"{v}_raw{a}_{lo}", [P, PACK, hi - lo], F32)
+            nc.sync.dma_start(
+                rows[:], hbm[v][4 * P * a : 4 * P * (a + 1), lo:hi].rearrange("(p j) s -> p j s", j=PACK)
+            )
+            raw[v, a, lo] = rows[:]
+            make_piece(v, a, lo, hi)
 
         tab_scale_rows = tab[:, 4 * P * T :].rearrange("a (quad row t) -> row quad a t", quad=4, row=4)
         w4_scale_rows = w4_scales.rearrange("a (quad row) n -> row quad a n", row=4)
 
-        def load_tab_scales(queue):
-            for row in range(4):
+        def load_tab_scales(queue, rows=range(4)):
+            for row in rows:
                 queue.dma_start(
                     ts[row : P : 32, :].rearrange("q (a t) -> q a t", a=PASSES).bitcast(I32),
                     tab_scale_rows[row].bitcast(I32),
                 )
 
-        def load_w4_scales(queue):
-            for row in range(4):
+        def load_w4_scales(queue, rows=range(4)):
+            for row in rows:
                 queue.dma_start(
                     ws[row : P : 32, :].rearrange("q (a n) -> q a n", a=PASSES).bitcast(I32),
                     w4_scale_rows[row].bitcast(I32),
                 )
 
-        def load_w4(lo, hi, queue=nc.sync):
-            queue.dma_start(ww[:, lo:hi, :].bitcast(I32), w4_words[lo:hi].rearrange("a p b -> p a b").bitcast(I32))
+        def load_w4(lo, hi):
+            nc.sync.dma_start(ww[:, lo:hi, :].bitcast(I32), w4_words[lo:hi].rearrange("a p b -> p a b").bitcast(I32))
 
-        def load_r(queue=nc.sync):
-            for m in range(2):
-                queue.dma_start(rs[m][:], r[P * m : P * (m + 1), :])
-
-        load_w4_scales(nc.gpsimd)
-        load_tab(0)
-        nc.sync.dma_start(offsets[:], offs)
-        load_raw("x", 0)
-        load_tab_scales(nc.sync)
-        load_raw("u", 0)
-        load_tab(1)
-        load_raw("x", 1)
-        load_tab(2)
-        load_raw("u", 1, 0, P)
-        load_raw("u", 1, P, S)
-        load_w4(0, 1)
-        load_w4(1, 2)
-        load_raw("u", 2, 0, P)
-        load_raw("x", 2, 0, P)
-        load_raw("x", 2, P, S)
-        load_raw("u", 2, P, S)
-        load_w4(2, 3)
-        load_r()
+        def load_r():
+            nc.sync.dma_start(rs[:], r.rearrange("(m p) s -> p m s", p=P))
 
         def interleave(engine, v, a, base, lo, hi):
             dst = grouped[v, a, base][:, lo:hi, :].rearrange("p (c i) t -> p c t i", i=4)
@@ -121,8 +112,8 @@ def tile_list_tabx_res_kernel(tc, tab, w4_words, w4_scales, x, u, r, offs, out):
                 in_=grouped[v, a, base][:].rearrange("p s t -> p (s t)"),
             )
 
-        def pick_words(a, lo=0, hi=S):
-            nc.vector.tensor_copy(gw[a][:, lo:hi], tw[a][:].bitcast(U32).indirect(offsets[:, lo // 16 : hi // 16]))
+        def pick_words(a):
+            nc.vector.tensor_copy(gw[a][:], tw[a].bitcast(U32).indirect(offsets[:]))
 
         def pick_scales(a):
             nc.vector.tensor_copy(gs[a][:], ts[:, T * a : T * (a + 1)].indirect(offsets[:]))
@@ -155,34 +146,51 @@ def tile_list_tabx_res_kernel(tc, tab, w4_words, w4_scales, x, u, r, offs, out):
 
         def add(m, h):
             hc = slice(P * h, P * (h + 1))
-            nc.vector.tensor_tensor(res[m][:, hc], acc[m, h][:], rs[m][:, hc], ADD)
+            nc.vector.tensor_tensor(res[m][:, hc], acc[m, h][:], rs[:, m, hc], ADD)
 
-        def store(m, queue):
-            queue.dma_start(out[P * m : P * (m + 1), :], res[m][:])
+        def store(m, lo=0, hi=S):
+            nc.sync.dma_start(out[P * m : P * (m + 1), lo:hi], res[m][:, lo:hi])
 
         four = [(m, h) for m in range(2) for h in range(2)]
+        nc.vector.memset(ws[:].bitcast(I32), 0)
+        nc.vector.memset(ts[:].bitcast(I32), 0)
+        load_w4_scales(nc.gpsimd, range(2))
+        load_tab(0, 1)
+        nc.sync.dma_start(offsets[:], offs)
+        load_passes("x", 0, 1)
+        load_passes("u", 0, 1)
+        load_tab_scales(nc.sync)
+        load_tab(1, 3)
+        load_passes("x", 1, 2)
+        load_w4_scales(nc.sync, range(2, 4))
+        load_passes("u", 1, 2)
+        load_w4(0, 1)
+        load_columns("u", 2, 0, P)
+        load_columns("x", 2, 0, P)
+        load_columns("x", 2, P, S)
+        load_columns("u", 2, P, S)
+        load_w4(1, 2)
+        load_w4(2, 3)
+        load_r()
+
         pick_words(0)
         interleave("S", "x", 0, 0, 0, S)
-        pick_scales(0)
-        pick_scales(1)
-        pick_scales(2)
         quantize("x", 0)
         interleave("S", "u", 0, 0, 0, S)
-        pick_words(1)
+        for a in range(PASSES):
+            pick_scales(a)
         quantize("u", 0)
-        for m, h in four:
-            own(0, m, h, True, False)
+        pick_words(1)
+        pick_words(2)
         interleave("S", "x", 1, 0, 0, S)
         quantize("x", 1)
-        pick_words(2)
         for m, h in four:
-            memory(0, m, h, False, False)
+            memory(0, m, h, True, False)
         for m, h in four:
-            memory(1, m, h, False, False)
-        interleave("S", "u", 1, 0, 0, P)
-        interleave("S", "u", 1, P, 0, P)
-        quantize("u", 1, 0)
-        quantize("u", 1, P)
+            own(0, m, h, False, False)
+        interleave("S", "u", 1, 0, 0, 192)
+        interleave("V", "u", 1, 0, 192, S)
+        quantize("u", 1)
         for m, h in four:
             own(1, m, h, False, False)
         interleave("S", "u", 2, 0, 0, P)
@@ -194,17 +202,19 @@ def tile_list_tabx_res_kernel(tc, tab, w4_words, w4_scales, x, u, r, offs, out):
         interleave("S", "u", 2, P, 0, 40)
         interleave("V", "u", 2, P, 40, P)
         quantize("x", 2, P)
+        for m, h in four:
+            memory(1, m, h, False, False)
         memory(2, 0, 0, False, True)
         memory(2, 0, 1, False, False)
+        own(2, 0, 1, False, True)
         memory(2, 1, 0, False, False)
         memory(2, 1, 1, False, False)
-        own(2, 0, 1, False, True)
         quantize("u", 2, P)
         own(2, 1, 0, False, True)
         own(2, 1, 1, False, True)
         add(0, 0)
         add(0, 1)
-        store(0, nc.sync)
-        add(1, 0)
-        add(1, 1)
-        store(1, nc.sync)
+        store(0)
+        for h in range(2):
+            add(1, h)
+            store(1, P * h, P * (h + 1))

@@ -26,7 +26,7 @@ def tile_list_tabx_res_kernel(tc, tab, w4_words, w4_scales, x, u, r, offs, out):
         psum = ctx.enter_context(tc.psum_pool(name="psum", bufs=1))
 
         def sb(name, shape, dtype):
-            return pool.tile(shape, dtype, name=name, align_bytes=64)
+            return pool.tile(shape, dtype, name=name, align_bytes=256)
 
         offsets = pool.tile([P, S // 16], U16, name="offsets")
         ts = sb("tab_scales", [P, PASSES * T], U8)
@@ -158,8 +158,8 @@ def tile_list_tabx_res_kernel(tc, tab, w4_words, w4_scales, x, u, r, offs, out):
         load_tab(0, 1)
         nc.sync.dma_start(offsets[:], offs)
         load_passes("x", 0, 1)
-        load_passes("u", 0, 1)
         load_tab_scales(nc.sync)
+        load_passes("u", 0, 1)
         load_tab(1, 3)
         load_passes("x", 1, 2)
         load_w4_scales(nc.sync, range(2, 4))
@@ -175,12 +175,12 @@ def tile_list_tabx_res_kernel(tc, tab, w4_words, w4_scales, x, u, r, offs, out):
 
         pick_words(0)
         interleave("S", "x", 0, 0, 0, S)
-        quantize("x", 0)
-        interleave("S", "u", 0, 0, 0, S)
         for a in range(PASSES):
             pick_scales(a)
-        quantize("u", 0)
+        quantize("x", 0)
+        interleave("S", "u", 0, 0, 0, S)
         pick_words(1)
+        quantize("u", 0)
         pick_words(2)
         interleave("S", "x", 1, 0, 0, S)
         quantize("x", 1)

@@ -28,14 +28,17 @@ def tile_list_tabx_res_kernel(tc, tab, w4_words, w4_scales, x, u, r, offs, out):
         def sb(name, shape, dtype):
             return pool.tile(shape, dtype, name=name, align_bytes=256)
 
+        def moved(name, shape, dtype):
+            return pool.tile(shape, dtype, name=name, align_bytes=4096)
+
         offsets = pool.tile([P, S // 16], U16, name="offsets")
-        ts = sb("tab_scales", [P, PASSES * T], U8)
-        ww = sb("w4_words_sb", [P, PASSES, 2 * M], U8)
-        ws = sb("w4_scales_sb", [P, PASSES * M], U8)
+        ts = moved("tab_scales", [P, PASSES * T], U8)
+        ww = moved("w4_words_sb", [P, PASSES, 2 * M], U8)
+        ws = moved("w4_scales_sb", [P, PASSES * M], U8)
         gw = [sb(f"picked_words{a}", [P, S], U32) for a in range(PASSES)]
         gs = [sb(f"picked_scales{a}", [P, S], U8) for a in range(PASSES)]
-        rs = sb("r_sb", [P, 2, S], F32)
-        res = [sb(f"result{m}", [P, S], F32) for m in range(2)]
+        rs = moved("r_sb", [P, 2, S], F32)
+        res = [moved(f"result{m}", [P, S], F32) for m in range(2)]
         acc = {(m, h): psum.tile([P, P], F32, name=f"acc{m}{h}") for m in range(2) for h in range(2)}
         hbm = {"x": x, "u": u}
         tw = {}
@@ -45,7 +48,7 @@ def tile_list_tabx_res_kernel(tc, tab, w4_words, w4_scales, x, u, r, offs, out):
         scales = {}
 
         def load_tab(lo, hi):
-            words = sb(f"tab_words{lo}", [P, hi - lo, T], I32)
+            words = moved(f"tab_words{lo}", [P, hi - lo, T], I32)
             nc.sync.dma_start(
                 words[:], tab[lo:hi, 0 : 4 * P * T].rearrange("a (p b) -> p a b", p=P).bitcast(I32)
             )
@@ -58,7 +61,7 @@ def tile_list_tabx_res_kernel(tc, tab, w4_words, w4_scales, x, u, r, offs, out):
             scales[v, a, lo] = sb(f"{v}_scales{a}_{lo}", [P, hi - lo], U8)
 
         def load_passes(v, lo, hi):
-            rows = sb(f"{v}_raw{lo}", [P, hi - lo, PACK * S], F32)
+            rows = moved(f"{v}_raw{lo}", [P, hi - lo, PACK * S], F32)
             nc.sync.dma_start(
                 rows[:], hbm[v][4 * P * lo : 4 * P * hi, :].rearrange("(a p j) s -> p a (j s)", p=P, j=PACK)
             )
@@ -67,7 +70,7 @@ def tile_list_tabx_res_kernel(tc, tab, w4_words, w4_scales, x, u, r, offs, out):
                 make_piece(v, a, 0, S)
 
         def load_columns(v, a, lo, hi):
-            rows = sb(f"{v}_raw{a}_{lo}", [P, PACK, hi - lo], F32)
+            rows = moved(f"{v}_raw{a}_{lo}", [P, PACK, hi - lo], F32)
             nc.sync.dma_start(
                 rows[:], hbm[v][4 * P * a : 4 * P * (a + 1), lo:hi].rearrange("(p j) s -> p j s", j=PACK)
             )

@@ -17,38 +17,50 @@ U8 = mybir.dt.uint8
 FP8X4 = mybir.dt.float8_e4m3fn_x4
 FP4X4 = mybir.dt.float4_e2m1fn_x4
 ADD = mybir.AluOpType.add
+AT = {
+    "x_raw2": 0,
+    "picked_scales": 3840,
+    "u_raw2_0": 4096,
+    "x_raw0": 6144,
+    "u_raw2_128": 6144,
+    "w4_words2": 8192,
+    "r_sb0": 8704,
+    "tab_scales": 14336,
+    "picked_words0": 14336,
+}
 
 
 def tile_list_tabx_res_kernel(tc, tab, w4_words, w4_scales, x, u, r, offs, out):
     nc = tc.nc
     with ExitStack() as ctx:
         pool = ctx.enter_context(tc.tile_pool(name="keep", bufs=1))
+        shared = ctx.enter_context(tc.tile_pool(name="shared", bufs=1))
         psum = ctx.enter_context(tc.psum_pool(name="psum", bufs=1))
 
         def sb(name, shape, dtype):
+            if name in AT:
+                return shared.tile(shape, dtype, name=name, align_bytes=256, offset=AT[name])
             return pool.tile(shape, dtype, name=name, align_bytes=256)
 
-        def moved(name, shape, dtype):
-            return pool.tile(shape, dtype, name=name, align_bytes=4096)
-
         offsets = pool.tile([P, S // 16], U16, name="offsets")
-        ts = moved("tab_scales", [P, PASSES * T], U8)
-        ww = moved("w4_words_sb", [P, PASSES, 2 * M], U8)
-        ws = moved("w4_scales_sb", [P, PASSES * M], U8)
+        ts = sb("tab_scales", [P, PASSES * T], U8)
+        planes = sb("planes", [P, PASSES * (S + M)], U8)
+        ws = planes[:, PASSES * S :]
         gw = [sb(f"picked_words{a}", [P, S], U32) for a in range(PASSES)]
-        gs = [sb(f"picked_scales{a}", [P, S], U8) for a in range(PASSES)]
-        rs = moved("r_sb", [P, 2, S], F32)
-        res = [moved(f"result{m}", [P, S], F32) for m in range(2)]
+        gs = sb("picked_scales", [P, PASSES * S], U8)
+        res = [sb(f"result{m}", [P, S], F32) for m in range(2)]
         acc = {(m, h): psum.tile([P, P], F32, name=f"acc{m}{h}") for m in range(2) for h in range(2)}
         hbm = {"x": x, "u": u}
         tw = {}
+        ww = {}
+        rs = {}
         raw = {}
         grouped = {}
         codes = {}
         scales = {}
 
         def load_tab(lo, hi):
-            words = moved(f"tab_words{lo}", [P, hi - lo, T], I32)
+            words = sb(f"tab_words{lo}", [P, hi - lo, T], I32)
             nc.sync.dma_start(
                 words[:], tab[lo:hi, 0 : 4 * P * T].rearrange("a (p b) -> p a b", p=P).bitcast(I32)
             )
@@ -60,45 +72,54 @@ def tile_list_tabx_res_kernel(tc, tab, w4_words, w4_scales, x, u, r, offs, out):
             codes[v, a, lo] = sb(f"{v}_codes{a}_{lo}", [P, hi - lo], U32)
             scales[v, a, lo] = sb(f"{v}_scales{a}_{lo}", [P, hi - lo], U8)
 
-        def load_passes(v, lo, hi):
-            rows = moved(f"{v}_raw{lo}", [P, hi - lo, PACK * S], F32)
+        def load_passes(v, lo, hi, width=S):
+            rows = sb(f"{v}_raw{lo}", [P, hi - lo, PACK * S], F32)
             nc.sync.dma_start(
                 rows[:], hbm[v][4 * P * lo : 4 * P * hi, :].rearrange("(a p j) s -> p a (j s)", p=P, j=PACK)
             )
             for a in range(lo, hi):
-                raw[v, a, 0] = rows[:, a - lo, :].rearrange("p (j s) -> p j s", j=PACK)
-                make_piece(v, a, 0, S)
+                for base in range(0, S, width):
+                    raw[v, a, base] = rows[:, a - lo, :].rearrange("p (j s) -> p j s", j=PACK)[:, :, base : base + width]
+                    make_piece(v, a, base, base + width)
 
         def load_columns(v, a, lo, hi):
-            rows = moved(f"{v}_raw{a}_{lo}", [P, PACK, hi - lo], F32)
+            rows = sb(f"{v}_raw{a}_{lo}", [P, PACK, hi - lo], F32)
             nc.sync.dma_start(
                 rows[:], hbm[v][4 * P * a : 4 * P * (a + 1), lo:hi].rearrange("(p j) s -> p j s", j=PACK)
             )
             raw[v, a, lo] = rows[:]
             make_piece(v, a, lo, hi)
 
-        tab_scale_rows = tab[:, 4 * P * T :].rearrange("a (quad row t) -> row quad a t", quad=4, row=4)
-        w4_scale_rows = w4_scales.rearrange("a (quad row) n -> row quad a n", row=4)
+        def load_tab_scales():
+            nc.sync.dma_start(
+                ts[0:P:8, :].rearrange("q (a t) -> q a t", a=PASSES).bitcast(I32),
+                tab[:, 4 * P * T :].rearrange("a (q t) -> q a t", q=16).bitcast(I32),
+            )
 
-        def load_tab_scales(queue, rows=range(4)):
-            for row in rows:
-                queue.dma_start(
-                    ts[row : P : 32, :].rearrange("q (a t) -> q a t", a=PASSES).bitcast(I32),
-                    tab_scale_rows[row].bitcast(I32),
-                )
+        def load_w4_scales():
+            nc.sync.dma_start(
+                planes[0:P:8, PASSES * S :].rearrange("q (a n) -> q a n", a=PASSES).bitcast(I32),
+                w4_scales.rearrange("a q n -> q a n").bitcast(I32),
+            )
 
-        def load_w4_scales(queue, rows=range(4)):
-            for row in rows:
-                queue.dma_start(
-                    ws[row : P : 32, :].rearrange("q (a n) -> q a n", a=PASSES).bitcast(I32),
-                    w4_scale_rows[row].bitcast(I32),
-                )
+        def join_planes():
+            nc.vector.tensor_copy(planes[:, 0 : PASSES * S].bitcast(I32), gs[:].bitcast(I32))
+
+        def place_scale_rows():
+            for row in range(1, 4):
+                nc.sync.dma_start(planes[row:P:32, :].bitcast(I32), planes[8 * row : P : 32, :].bitcast(I32))
 
         def load_w4(lo, hi):
-            nc.sync.dma_start(ww[:, lo:hi, :].bitcast(I32), w4_words[lo:hi].rearrange("a p b -> p a b").bitcast(I32))
+            words = sb(f"w4_words{lo}", [P, hi - lo, 2 * M], U8)
+            nc.sync.dma_start(words[:].bitcast(I32), w4_words[lo:hi].rearrange("a p b -> p a b").bitcast(I32))
+            for a in range(lo, hi):
+                ww[a] = words[:, a - lo, :]
 
-        def load_r():
-            nc.sync.dma_start(rs[:], r.rearrange("(m p) s -> p m s", p=P))
+        def load_r(lo, hi):
+            rows = sb(f"r_sb{lo}", [P, hi - lo, S], F32)
+            nc.sync.dma_start(rows[:], r[P * lo : P * hi, :].rearrange("(m p) s -> p m s", p=P))
+            for m in range(lo, hi):
+                rs[m] = rows[:, m - lo, :]
 
         def interleave(engine, v, a, base, lo, hi):
             dst = grouped[v, a, base][:, lo:hi, :].rearrange("p (c i) t -> p c t i", i=4)
@@ -119,7 +140,7 @@ def tile_list_tabx_res_kernel(tc, tab, w4_words, w4_scales, x, u, r, offs, out):
             nc.vector.tensor_copy(gw[a][:], tw[a].bitcast(U32).indirect(offsets[:]))
 
         def pick_scales(a):
-            nc.vector.tensor_copy(gs[a][:], ts[:, T * a : T * (a + 1)].indirect(offsets[:]))
+            nc.vector.tensor_copy(gs[:, S * a : S * (a + 1)], ts[:, T * a : T * (a + 1)].indirect(offsets[:]))
 
         def operand(v, a, half):
             if (v, a, P) in codes:
@@ -141,80 +162,72 @@ def tile_list_tabx_res_kernel(tc, tab, w4_words, w4_scales, x, u, r, offs, out):
             hc = slice(P * h, P * (h + 1))
             nc.tensor.matmul_mx(
                 out=acc[m, h][:],
-                lhsT=ww[:, a, 2 * P * m : 2 * P * (m + 1)].bitcast(FP4X4),
+                lhsT=ww[a][:, 2 * P * m : 2 * P * (m + 1)].bitcast(FP4X4),
                 lhsT_scale=ws[:, M * a + P * m : M * a + P * (m + 1)],
-                rhs=gw[a][:, hc].bitcast(FP8X4), rhs_scale=gs[a][:, hc],
+                rhs=gw[a][:, hc].bitcast(FP8X4), rhs_scale=planes[:, S * a + P * h : S * a + P * (h + 1)],
                 start=start, stop=stop,
             )
 
         def add(m, h):
             hc = slice(P * h, P * (h + 1))
-            nc.vector.tensor_tensor(res[m][:, hc], acc[m, h][:], rs[:, m, hc], ADD)
+            nc.vector.tensor_tensor(res[m][:, hc], acc[m, h][:], rs[m][:, hc], ADD)
 
         def store(m, lo=0, hi=S):
             nc.sync.dma_start(out[P * m : P * (m + 1), lo:hi], res[m][:, lo:hi])
 
         four = [(m, h) for m in range(2) for h in range(2)]
-        nc.vector.memset(ws[:].bitcast(I32), 0)
         nc.vector.memset(ts[:].bitcast(I32), 0)
-        load_w4_scales(nc.gpsimd, range(2))
+        nc.vector.memset(ws.bitcast(I32), 0)
         load_tab(0, 1)
         nc.sync.dma_start(offsets[:], offs)
-        load_passes("x", 0, 1)
-        load_tab_scales(nc.sync)
+        load_w4(0, 2)
+        load_tab_scales()
+        load_w4_scales()
+        load_passes("x", 0, 2)
         load_passes("u", 0, 1)
         load_tab(1, 3)
-        load_passes("x", 1, 2)
-        load_w4_scales(nc.sync, range(2, 4))
         load_passes("u", 1, 2)
-        load_w4(0, 1)
-        load_columns("u", 2, 0, P)
-        load_columns("x", 2, 0, P)
-        load_columns("x", 2, P, S)
-        load_columns("u", 2, P, S)
-        load_w4(1, 2)
-        load_w4(2, 3)
-        load_r()
-
-        pick_words(0)
-        interleave("S", "x", 0, 0, 0, S)
         for a in range(PASSES):
             pick_scales(a)
-        quantize("x", 0)
-        interleave("S", "u", 0, 0, 0, S)
-        pick_words(1)
-        quantize("u", 0)
-        pick_words(2)
+        join_planes()
+        place_scale_rows()
+        load_passes("x", 2, 3, P)
+        load_columns("u", 2, 0, P)
+        interleave("S", "x", 0, 0, 0, S)
         interleave("S", "x", 1, 0, 0, S)
+        load_columns("u", 2, P, S)
+        load_w4(2, 3)
+        load_r(0, 2)
+        pick_words(0)
+        quantize("x", 0)
+        pick_words(1)
         quantize("x", 1)
-        for m, h in four:
-            memory(0, m, h, True, False)
-        for m, h in four:
-            own(0, m, h, False, False)
+        pick_words(2)
+        interleave("S", "u", 0, 0, 0, S)
+        quantize("u", 0)
         interleave("S", "u", 1, 0, 0, 192)
         interleave("V", "u", 1, 0, 192, S)
+        for a in range(2):
+            for m, h in four:
+                memory(a, m, h, a == 0, False)
+        for m, h in four:
+            own(0, m, h, False, False)
+        interleave("V", "x", 2, P, 0, P)
         quantize("u", 1)
         for m, h in four:
             own(1, m, h, False, False)
-        interleave("S", "u", 2, 0, 0, P)
-        interleave("V", "x", 2, 0, 0, P)
-        quantize("u", 2, 0)
+        interleave("S", "x", 2, 0, 0, P)
+        quantize("x", 2, P)
         quantize("x", 2, 0)
-        own(2, 0, 0, False, False)
-        interleave("S", "x", 2, P, 0, P)
+        interleave("S", "u", 2, 0, 0, P)
         interleave("S", "u", 2, P, 0, 40)
         interleave("V", "u", 2, P, 40, P)
-        quantize("x", 2, P)
-        for m, h in four:
-            memory(1, m, h, False, False)
-        memory(2, 0, 0, False, True)
-        memory(2, 0, 1, False, False)
-        own(2, 0, 1, False, True)
-        memory(2, 1, 0, False, False)
-        memory(2, 1, 1, False, False)
+        quantize("u", 2, 0)
         quantize("u", 2, P)
-        own(2, 1, 0, False, True)
-        own(2, 1, 1, False, True)
+        for m, h in four:
+            memory(2, m, h, False, False)
+        for m, h in four:
+            own(2, m, h, False, True)
         add(0, 0)
         add(0, 1)
         store(0)

@@ -18,15 +18,19 @@ FP8X4 = mybir.dt.float8_e4m3fn_x4
 FP4X4 = mybir.dt.float4_e2m1fn_x4
 ADD = mybir.AluOpType.add
 AT = {
-    "x_raw2": 0,
-    "picked_scales": 3840,
-    "u_raw2_0": 4096,
-    "x_raw0": 6144,
+    "u_raw2_0": 0,
+    "picked_scales": 1792,
+    "x_raw2_0": 2048,
+    "u_raw0": 4096,
+    "x_raw2_128": 4096,
     "u_raw2_128": 6144,
-    "w4_words2": 8192,
-    "r_sb0": 8704,
+    "x_raw1": 8192,
+    "w4_words1": 8192,
+    "r_sb0": 9216,
     "tab_scales": 14336,
     "picked_words0": 14336,
+    "w4_words2": 8704,
+    "r_sb1": 10240,
 }
 
 
@@ -180,54 +184,63 @@ def tile_list_tabx_res_kernel(tc, tab, w4_words, w4_scales, x, u, r, offs, out):
         nc.vector.memset(ws.bitcast(I32), 0)
         load_tab(0, 1)
         nc.sync.dma_start(offsets[:], offs)
-        load_w4(0, 2)
+        load_w4(0, 1)
         load_tab_scales()
+        load_passes("x", 0, 1)
         load_w4_scales()
-        load_passes("x", 0, 2)
         load_passes("u", 0, 1)
         load_tab(1, 3)
+        load_passes("x", 1, 2)
         load_passes("u", 1, 2)
         for a in range(PASSES):
             pick_scales(a)
         join_planes()
         place_scale_rows()
-        load_passes("x", 2, 3, P)
         load_columns("u", 2, 0, P)
+        load_columns("x", 2, 0, P)
         interleave("S", "x", 0, 0, 0, S)
-        interleave("S", "x", 1, 0, 0, S)
+        interleave("S", "u", 0, 0, 0, S)
+        load_columns("x", 2, P, S)
         load_columns("u", 2, P, S)
+        interleave("S", "x", 1, 0, 0, S)
+        load_w4(1, 2)
         load_w4(2, 3)
-        load_r(0, 2)
+        load_r(0, 1)
+        load_r(1, 2)
         pick_words(0)
         quantize("x", 0)
-        pick_words(1)
-        quantize("x", 1)
-        pick_words(2)
-        interleave("S", "u", 0, 0, 0, S)
         quantize("u", 0)
-        interleave("S", "u", 1, 0, 0, 192)
-        interleave("V", "u", 1, 0, 192, S)
-        for a in range(2):
-            for m, h in four:
-                memory(a, m, h, a == 0, False)
+        pick_words(1)
+        pick_words(2)
+        quantize("x", 1)
         for m, h in four:
-            own(0, m, h, False, False)
-        interleave("V", "x", 2, P, 0, P)
+            own(0, m, h, True, False)
+        for m, h in four:
+            memory(0, m, h, False, False)
+        interleave("S", "u", 1, 0, 0, P)
+        interleave("V", "u", 1, 0, P, S)
         quantize("u", 1)
         for m, h in four:
             own(1, m, h, False, False)
-        interleave("S", "x", 2, 0, 0, P)
-        quantize("x", 2, P)
-        quantize("x", 2, 0)
         interleave("S", "u", 2, 0, 0, P)
+        interleave("V", "x", 2, 0, 0, P)
+        quantize("u", 2, 0)
+        quantize("x", 2, 0)
+        own(2, 0, 0, False, False)
+        interleave("S", "x", 2, P, 0, P)
         interleave("S", "u", 2, P, 0, 40)
         interleave("V", "u", 2, P, 40, P)
-        quantize("u", 2, 0)
+        quantize("x", 2, P)
+        for m, h in four:
+            memory(1, m, h, False, False)
+        memory(2, 0, 0, False, True)
+        memory(2, 0, 1, False, False)
+        own(2, 0, 1, False, True)
+        memory(2, 1, 0, False, False)
+        memory(2, 1, 1, False, False)
         quantize("u", 2, P)
-        for m, h in four:
-            memory(2, m, h, False, False)
-        for m, h in four:
-            own(2, m, h, False, True)
+        own(2, 1, 0, False, True)
+        own(2, 1, 1, False, True)
         add(0, 0)
         add(0, 1)
         store(0)

@@ -27,10 +27,12 @@ AT = {
     "x_raw1": 8192,
     "w4_words1": 8192,
     "r_sb0": 9216,
-    "tab_scales": 14336,
+    "tab_scales": 15104,
     "picked_words0": 14336,
     "w4_words2": 8704,
     "r_sb1": 10240,
+    "picked_words1": 15360,
+    "picked_words2": 16384,
 }
 
 
@@ -176,20 +178,19 @@ def tile_list_tabx_res_kernel(tc, tab, w4_words, w4_scales, x, u, r, offs, out):
             hc = slice(P * h, P * (h + 1))
             nc.vector.tensor_tensor(res[m][:, hc], acc[m, h][:], rs[m][:, hc], ADD)
 
-        def store(m, lo=0, hi=S):
-            nc.sync.dma_start(out[P * m : P * (m + 1), lo:hi], res[m][:, lo:hi])
+        def store(m, lo=0, hi=S, queue=nc.sync):
+            queue.dma_start(out[P * m : P * (m + 1), lo:hi], res[m][:, lo:hi])
 
         four = [(m, h) for m in range(2) for h in range(2)]
         nc.vector.memset(ts[:].bitcast(I32), 0)
         nc.vector.memset(ws.bitcast(I32), 0)
-        load_tab(0, 1)
+        load_passes("x", 0, 1)
         nc.sync.dma_start(offsets[:], offs)
         load_w4(0, 1)
         load_tab_scales()
-        load_passes("x", 0, 1)
+        load_tab(0, 3)
         load_w4_scales()
         load_passes("u", 0, 1)
-        load_tab(1, 3)
         load_passes("x", 1, 2)
         load_passes("u", 1, 2)
         for a in range(PASSES):
@@ -207,16 +208,16 @@ def tile_list_tabx_res_kernel(tc, tab, w4_words, w4_scales, x, u, r, offs, out):
         load_w4(2, 3)
         load_r(0, 1)
         load_r(1, 2)
-        pick_words(0)
         quantize("x", 0)
-        quantize("u", 0)
+        pick_words(0)
         pick_words(1)
+        quantize("u", 0)
         pick_words(2)
         quantize("x", 1)
         for m, h in four:
-            own(0, m, h, True, False)
+            memory(0, m, h, True, False)
         for m, h in four:
-            memory(0, m, h, False, False)
+            own(0, m, h, False, False)
         interleave("S", "u", 1, 0, 0, P)
         interleave("V", "u", 1, 0, P, S)
         quantize("u", 1)
@@ -231,19 +232,18 @@ def tile_list_tabx_res_kernel(tc, tab, w4_words, w4_scales, x, u, r, offs, out):
         interleave("S", "u", 2, P, 0, 40)
         interleave("V", "u", 2, P, 40, P)
         quantize("x", 2, P)
-        for m, h in four:
-            memory(1, m, h, False, False)
+        memory(1, 0, 0, False, False)
+        memory(1, 0, 1, False, False)
         memory(2, 0, 0, False, True)
         memory(2, 0, 1, False, False)
+        memory(1, 1, 0, False, False)
         own(2, 0, 1, False, True)
         memory(2, 1, 0, False, False)
+        memory(1, 1, 1, False, False)
         memory(2, 1, 1, False, False)
         quantize("u", 2, P)
         own(2, 1, 0, False, True)
         own(2, 1, 1, False, True)
-        add(0, 0)
-        add(0, 1)
-        store(0)
-        for h in range(2):
-            add(1, h)
-            store(1, P * h, P * (h + 1))
+        for m, h in four:
+            add(m, h)
+            store(m, P * h, P * (h + 1), nc.sync if h else nc.scalar)

@@ -215,9 +215,9 @@ def tile_list_tabx_res_kernel(tc, tab, w4_words, w4_scales, x, u, r, offs, out):
         pick_words(2)
         quantize("x", 1)
         for m, h in four:
-            memory(0, m, h, True, False)
+            own(0, m, h, True, False)
         for m, h in four:
-            own(0, m, h, False, False)
+            memory(0, m, h, False, False)
         interleave("S", "u", 1, 0, 0, P)
         interleave("V", "u", 1, 0, P, S)
         quantize("u", 1)

@@ -30,9 +30,10 @@ AT = {
     "tab_scales": 15104,
     "picked_words0": 14336,
     "w4_words2": 8704,
-    "r_sb1": 10240,
     "picked_words1": 15360,
     "picked_words2": 16384,
+    "r_sb1_0": 10240,
+    "r_sb1_1": 10752,
 }
 
 
@@ -50,8 +51,8 @@ def tile_list_tabx_res_kernel(tc, tab, w4_words, w4_scales, x, u, r, offs, out):
 
         offsets = pool.tile([P, S // 16], U16, name="offsets")
         ts = sb("tab_scales", [P, PASSES * T], U8)
-        planes = sb("planes", [P, PASSES * (S + M)], U8)
-        ws = planes[:, PASSES * S :]
+        planes = sb("planes", [P, PASSES * S], U8)
+        ws = sb("w4_scales_sb", [P, PASSES * M], U8)
         gw = [sb(f"picked_words{a}", [P, S], U32) for a in range(PASSES)]
         gs = sb("picked_scales", [P, PASSES * S], U8)
         res = [sb(f"result{m}", [P, S], F32) for m in range(2)]
@@ -59,7 +60,7 @@ def tile_list_tabx_res_kernel(tc, tab, w4_words, w4_scales, x, u, r, offs, out):
         hbm = {"x": x, "u": u}
         tw = {}
         ww = {}
-        rs = {}
+        rq = {}
         raw = {}
         grouped = {}
         codes = {}
@@ -103,13 +104,14 @@ def tile_list_tabx_res_kernel(tc, tab, w4_words, w4_scales, x, u, r, offs, out):
             )
 
         def load_w4_scales():
-            nc.sync.dma_start(
-                planes[0:P:8, PASSES * S :].rearrange("q (a n) -> q a n", a=PASSES).bitcast(I32),
-                w4_scales.rearrange("a q n -> q a n").bitcast(I32),
-            )
+            rows = w4_scales.rearrange("a (quad row) n -> row quad a n", row=4)
+            for row in range(4):
+                nc.gpsimd.dma_start(
+                    ws[row:P:32, :].rearrange("q (a n) -> q a n", a=PASSES).bitcast(I32), rows[row].bitcast(I32)
+                )
 
         def join_planes():
-            nc.vector.tensor_copy(planes[:, 0 : PASSES * S].bitcast(I32), gs[:].bitcast(I32))
+            nc.vector.tensor_copy(planes[:].bitcast(I32), gs[:].bitcast(I32))
 
         def place_scale_rows():
             for row in range(1, 4):
@@ -125,7 +127,13 @@ def tile_list_tabx_res_kernel(tc, tab, w4_words, w4_scales, x, u, r, offs, out):
             rows = sb(f"r_sb{lo}", [P, hi - lo, S], F32)
             nc.sync.dma_start(rows[:], r[P * lo : P * hi, :].rearrange("(m p) s -> p m s", p=P))
             for m in range(lo, hi):
-                rs[m] = rows[:, m - lo, :]
+                for h in range(2):
+                    rq[m, h] = rows[:, m - lo, P * h : P * (h + 1)]
+
+        def load_r_quarter(m, h):
+            rows = sb(f"r_sb{m}_{h}", [P, P], F32)
+            nc.sync.dma_start(rows[:], r[P * m : P * (m + 1), P * h : P * (h + 1)])
+            rq[m, h] = rows[:]
 
         def interleave(engine, v, a, base, lo, hi):
             dst = grouped[v, a, base][:, lo:hi, :].rearrange("p (c i) t -> p c t i", i=4)
@@ -176,20 +184,20 @@ def tile_list_tabx_res_kernel(tc, tab, w4_words, w4_scales, x, u, r, offs, out):
 
         def add(m, h):
             hc = slice(P * h, P * (h + 1))
-            nc.vector.tensor_tensor(res[m][:, hc], acc[m, h][:], rs[m][:, hc], ADD)
+            nc.vector.tensor_tensor(res[m][:, hc], acc[m, h][:], rq[m, h], ADD)
 
         def store(m, lo=0, hi=S, queue=nc.sync):
             queue.dma_start(out[P * m : P * (m + 1), lo:hi], res[m][:, lo:hi])
 
         four = [(m, h) for m in range(2) for h in range(2)]
         nc.vector.memset(ts[:].bitcast(I32), 0)
-        nc.vector.memset(ws.bitcast(I32), 0)
+        nc.vector.memset(ws[:].bitcast(I32), 0)
+        load_w4_scales()
         load_passes("x", 0, 1)
         nc.sync.dma_start(offsets[:], offs)
         load_w4(0, 1)
         load_tab_scales()
         load_tab(0, 3)
-        load_w4_scales()
         load_passes("u", 0, 1)
         load_passes("x", 1, 2)
         load_passes("u", 1, 2)
@@ -207,7 +215,8 @@ def tile_list_tabx_res_kernel(tc, tab, w4_words, w4_scales, x, u, r, offs, out):
         load_w4(1, 2)
         load_w4(2, 3)
         load_r(0, 1)
-        load_r(1, 2)
+        load_r_quarter(1, 0)
+        load_r_quarter(1, 1)
         quantize("x", 0)
         pick_words(0)
         pick_words(1)
@@ -228,9 +237,10 @@ def tile_list_tabx_res_kernel(tc, tab, w4_words, w4_scales, x, u, r, offs, out):
         quantize("u", 2, 0)
         quantize("x", 2, 0)
         own(2, 0, 0, False, False)
-        interleave("S", "x", 2, P, 0, P)
-        interleave("S", "u", 2, P, 0, 40)
-        interleave("V", "u", 2, P, 40, P)
+        interleave("S", "x", 2, P, 0, 96)
+        interleave("V", "x", 2, P, 96, P)
+        interleave("S", "u", 2, P, 0, 48)
+        interleave("V", "u", 2, P, 48, P)
         quantize("x", 2, P)
         memory(1, 0, 0, False, False)
         memory(1, 0, 1, False, False)

@@ -18,23 +18,22 @@ FP8X4 = mybir.dt.float8_e4m3fn_x4
 FP4X4 = mybir.dt.float4_e2m1fn_x4
 ADD = mybir.AluOpType.add
 AT = {
+    "picked_scales": 0,
     "u_raw2_0": 0,
-    "picked_scales": 1792,
     "x_raw2_0": 2048,
-    "u_raw0": 4096,
     "x_raw2_128": 4096,
     "u_raw2_128": 6144,
-    "x_raw1": 8192,
     "w4_words1": 8192,
-    "r_sb0": 9216,
-    "tab_scales": 15104,
-    "picked_words0": 14336,
     "w4_words2": 8704,
-    "picked_words1": 15360,
-    "picked_words2": 16384,
+    "r_sb0": 9216,
     "r_sb1_0": 10240,
     "r_sb1_1": 10752,
+    "tab_scales": 15104,
+    "picked_words0": 14336,
+    "picked_words1": 15360,
+    "picked_words2": 16384,
 }
+LATE_BYTES = 11264
 
 
 def tile_list_tabx_res_kernel(tc, tab, w4_words, w4_scales, x, u, r, offs, out):
@@ -54,7 +53,7 @@ def tile_list_tabx_res_kernel(tc, tab, w4_words, w4_scales, x, u, r, offs, out):
         planes = sb("planes", [P, PASSES * S], U8)
         ws = sb("w4_scales_sb", [P, PASSES * M], U8)
         gw = [sb(f"picked_words{a}", [P, S], U32) for a in range(PASSES)]
-        gs = sb("picked_scales", [P, PASSES * S], U8)
+        gs = sb("picked_scales", [P, LATE_BYTES], U8)[:, 0 : PASSES * S]
         res = [sb(f"result{m}", [P, S], F32) for m in range(2)]
         acc = {(m, h): psum.tile([P, P], F32, name=f"acc{m}{h}") for m in range(2) for h in range(2)}
         hbm = {"x": x, "u": u}
@@ -111,7 +110,7 @@ def tile_list_tabx_res_kernel(tc, tab, w4_words, w4_scales, x, u, r, offs, out):
                 )
 
         def join_planes():
-            nc.vector.tensor_copy(planes[:].bitcast(I32), gs[:].bitcast(I32))
+            nc.vector.tensor_copy(planes[:].bitcast(I32), gs.bitcast(I32))
 
         def place_scale_rows():
             for row in range(1, 4):

from contextlib import ExitStack

import concourse.mybir as mybir

K, L, M, T, S = 1536, 1536, 256, 512, 256
P = 128
PACK = 4
PASSES = 3
FLOPS = 2 * (K + L) * M * S

F32 = mybir.dt.float32
BF16 = mybir.dt.bfloat16
I32 = mybir.dt.int32
U32 = mybir.dt.uint32
U16 = mybir.dt.uint16
U8 = mybir.dt.uint8
FP8X4 = mybir.dt.float8_e4m3fn_x4
FP4X4 = mybir.dt.float4_e2m1fn_x4
ADD = mybir.AluOpType.add
AT = {
    "picked_scales": 0,
    "u_raw2_0": 0,
    "x_raw2_0": 2048,
    "x_raw2_128": 4096,
    "u_raw2_128": 6144,
    "w4_words1": 8192,
    "w4_words2": 8704,
    "r_sb0": 9216,
    "r_sb1_0": 10240,
    "r_sb1_1": 10752,
    "tab_scales": 15104,
    "picked_words0": 14336,
    "picked_words1": 15360,
    "picked_words2": 16384,
}
LATE_BYTES = 11264


def tile_list_tabx_res_kernel(tc, tab, w4_words, w4_scales, x, u, r, offs, out):
    nc = tc.nc
    with ExitStack() as ctx:
        pool = ctx.enter_context(tc.tile_pool(name="keep", bufs=1))
        shared = ctx.enter_context(tc.tile_pool(name="shared", bufs=1))
        psum = ctx.enter_context(tc.psum_pool(name="psum", bufs=1))

        def sb(name, shape, dtype):
            if name in AT:
                return shared.tile(shape, dtype, name=name, align_bytes=256, offset=AT[name])
            return pool.tile(shape, dtype, name=name, align_bytes=256)

        offsets = pool.tile([P, S // 16], U16, name="offsets")
        ts = sb("tab_scales", [P, PASSES * T], U8)
        planes = sb("planes", [P, PASSES * S], U8)
        ws = sb("w4_scales_sb", [P, PASSES * M], U8)
        gw = [sb(f"picked_words{a}", [P, S], U32) for a in range(PASSES)]
        gs = sb("picked_scales", [P, LATE_BYTES], U8)[:, 0 : PASSES * S]
        res = [sb(f"result{m}", [P, S], F32) for m in range(2)]
        acc = {(m, h): psum.tile([P, P], F32, name=f"acc{m}{h}") for m in range(2) for h in range(2)}
        hbm = {"x": x, "u": u}
        tw = {}
        ww = {}
        rq = {}
        raw = {}
        grouped = {}
        codes = {}
        scales = {}

        def load_tab(lo, hi):
            words = sb(f"tab_words{lo}", [P, hi - lo, T], I32)
            nc.sync.dma_start(
                words[:], tab[lo:hi, 0 : 4 * P * T].rearrange("a (p b) -> p a b", p=P).bitcast(I32)
            )
            for a in range(lo, hi):
                tw[a] = words[:, a - lo, :]

        def make_piece(v, a, lo, hi):
            grouped[v, a, lo] = sb(f"{v}_grouped{a}_{lo}", [P, hi - lo, PACK], BF16)
            codes[v, a, lo] = sb(f"{v}_codes{a}_{lo}", [P, hi - lo], U32)
            scales[v, a, lo] = sb(f"{v}_scales{a}_{lo}", [P, hi - lo], U8)

        def load_passes(v, lo, hi, width=S):
            rows = sb(f"{v}_raw{lo}", [P, hi - lo, PACK * S], F32)
            nc.sync.dma_start(
                rows[:], hbm[v][4 * P * lo : 4 * P * hi, :].rearrange("(a p j) s -> p a (j s)", p=P, j=PACK)
            )
            for a in range(lo, hi):
                for base in range(0, S, width):
                    raw[v, a, base] = rows[:, a - lo, :].rearrange("p (j s) -> p j s", j=PACK)[:, :, base : base + width]
                    make_piece(v, a, base, base + width)

        def load_columns(v, a, lo, hi):
            rows = sb(f"{v}_raw{a}_{lo}", [P, PACK, hi - lo], F32)
            nc.sync.dma_start(
                rows[:], hbm[v][4 * P * a : 4 * P * (a + 1), lo:hi].rearrange("(p j) s -> p j s", j=PACK)
            )
            raw[v, a, lo] = rows[:]
            make_piece(v, a, lo, hi)

        def load_tab_scales():
            nc.sync.dma_start(
                ts[0:P:8, :].rearrange("q (a t) -> q a t", a=PASSES).bitcast(I32),
                tab[:, 4 * P * T :].rearrange("a (q t) -> q a t", q=16).bitcast(I32),
            )

        def load_w4_scales():
            rows = w4_scales.rearrange("a (quad row) n -> row quad a n", row=4)
            for row in range(4):
                nc.gpsimd.dma_start(
                    ws[row:P:32, :].rearrange("q (a n) -> q a n", a=PASSES).bitcast(I32), rows[row].bitcast(I32)
                )

        def join_planes():
            nc.vector.tensor_copy(planes[:].bitcast(I32), gs.bitcast(I32))

        def place_scale_rows():
            for row in range(1, 4):
                nc.sync.dma_start(planes[row:P:32, :].bitcast(I32), planes[8 * row : P : 32, :].bitcast(I32))

        def load_w4(lo, hi):
            words = sb(f"w4_words{lo}", [P, hi - lo, 2 * M], U8)
            nc.sync.dma_start(words[:].bitcast(I32), w4_words[lo:hi].rearrange("a p b -> p a b").bitcast(I32))
            for a in range(lo, hi):
                ww[a] = words[:, a - lo, :]

        def load_r(lo, hi):
            rows = sb(f"r_sb{lo}", [P, hi - lo, S], F32)
            nc.sync.dma_start(rows[:], r[P * lo : P * hi, :].rearrange("(m p) s -> p m s", p=P))
            for m in range(lo, hi):
                for h in range(2):
                    rq[m, h] = rows[:, m - lo, P * h : P * (h + 1)]

        def load_r_quarter(m, h):
            rows = sb(f"r_sb{m}_{h}", [P, P], F32)
            nc.sync.dma_start(rows[:], r[P * m : P * (m + 1), P * h : P * (h + 1)])
            rq[m, h] = rows[:]

        def interleave(engine, v, a, base, lo, hi):
            dst = grouped[v, a, base][:, lo:hi, :].rearrange("p (c i) t -> p c t i", i=4)
            src = raw[v, a, base][:, :, lo:hi].rearrange("p t (c i) -> p c t i", i=4)
            if engine == "S":
                nc.scalar.copy(dst, src)
            else:
                nc.vector.tensor_copy(dst, src)

        def quantize(v, a, base=0):
            nc.vector.quantize_mx(
                out=codes[v, a, base][:].bitcast(FP8X4),
                scales=scales[v, a, base][:],
                in_=grouped[v, a, base][:].rearrange("p s t -> p (s t)"),
            )

        def pick_words(a):
            nc.vector.tensor_copy(gw[a][:], tw[a].bitcast(U32).indirect(offsets[:]))

        def pick_scales(a):
            nc.vector.tensor_copy(gs[:, S * a : S * (a + 1)], ts[:, T * a : T * (a + 1)].indirect(offsets[:]))

        def operand(v, a, half):
            if (v, a, P) in codes:
                return codes[v, a, P * half][:], scales[v, a, P * half][:]
            cols = slice(P * half, P * (half + 1))
            return codes[v, a, 0][:, cols], scales[v, a, 0][:, cols]

        def own(a, m, h, start, stop):
            lc, ls = operand("u", a, m)
            rc, rscale = operand("x", a, h)
            nc.tensor.matmul_mx(
                out=acc[m, h][:],
                lhsT=lc.bitcast(FP8X4), lhsT_scale=ls,
                rhs=rc.bitcast(FP8X4), rhs_scale=rscale,
                start=start, stop=stop,
            )

        def memory(a, m, h, start, stop):
            hc = slice(P * h, P * (h + 1))
            nc.tensor.matmul_mx(
                out=acc[m, h][:],
                lhsT=ww[a][:, 2 * P * m : 2 * P * (m + 1)].bitcast(FP4X4),
                lhsT_scale=ws[:, M * a + P * m : M * a + P * (m + 1)],
                rhs=gw[a][:, hc].bitcast(FP8X4), rhs_scale=planes[:, S * a + P * h : S * a + P * (h + 1)],
                start=start, stop=stop,
            )

        def add(m, h):
            hc = slice(P * h, P * (h + 1))
            nc.vector.tensor_tensor(res[m][:, hc], acc[m, h][:], rq[m, h], ADD)

        def store(m, lo=0, hi=S, queue=nc.sync):
            queue.dma_start(out[P * m : P * (m + 1), lo:hi], res[m][:, lo:hi])

        four = [(m, h) for m in range(2) for h in range(2)]
        nc.vector.memset(ts[:].bitcast(I32), 0)
        nc.vector.memset(ws[:].bitcast(I32), 0)
        load_w4_scales()
        load_passes("x", 0, 1)
        nc.sync.dma_start(offsets[:], offs)
        load_w4(0, 1)
        load_tab_scales()
        load_tab(0, 3)
        load_passes("u", 0, 1)
        load_passes("x", 1, 2)
        load_passes("u", 1, 2)
        for a in range(PASSES):
            pick_scales(a)
        join_planes()
        place_scale_rows()
        load_columns("u", 2, 0, P)
        load_columns("x", 2, 0, P)
        interleave("S", "x", 0, 0, 0, S)
        interleave("S", "u", 0, 0, 0, S)
        load_columns("x", 2, P, S)
        load_columns("u", 2, P, S)
        interleave("S", "x", 1, 0, 0, S)
        load_w4(1, 2)
        load_w4(2, 3)
        load_r(0, 1)
        load_r_quarter(1, 0)
        load_r_quarter(1, 1)
        quantize("x", 0)
        pick_words(0)
        pick_words(1)
        quantize("u", 0)
        pick_words(2)
        quantize("x", 1)
        for m, h in four:
            own(0, m, h, True, False)
        for m, h in four:
            memory(0, m, h, False, False)
        interleave("S", "u", 1, 0, 0, P)
        interleave("V", "u", 1, 0, P, S)
        quantize("u", 1)
        for m, h in four:
            own(1, m, h, False, False)
        interleave("S", "u", 2, 0, 0, P)
        interleave("V", "x", 2, 0, 0, P)
        quantize("u", 2, 0)
        quantize("x", 2, 0)
        own(2, 0, 0, False, False)
        interleave("S", "x", 2, P, 0, 96)
        interleave("V", "x", 2, P, 96, P)
        interleave("S", "u", 2, P, 0, 48)
        interleave("V", "u", 2, P, 48, P)
        quantize("x", 2, P)
        memory(1, 0, 0, False, False)
        memory(1, 0, 1, False, False)
        memory(2, 0, 0, False, True)
        memory(2, 0, 1, False, False)
        memory(1, 1, 0, False, False)
        own(2, 0, 1, False, True)
        memory(2, 1, 0, False, False)
        memory(1, 1, 1, False, False)
        memory(2, 1, 1, False, False)
        quantize("u", 2, P)
        own(2, 1, 0, False, True)
        own(2, 1, 1, False, True)
        for m, h in four:
            add(m, h)
            store(m, P * h, P * (h + 1), nc.sync if h else nc.scalar)
